import numpy as np
import ml_dtypes


def mxq(x, axis, fmt="e4m3"):
    dtype, down = {"e4m3": (ml_dtypes.float8_e4m3fn, 7), "e5m2": (ml_dtypes.float8_e5m2, 14)}[fmt]
    v = np.moveaxis(np.asarray(x, np.float32).astype(ml_dtypes.bfloat16).astype(np.float64), axis, -1)
    blocks = v.reshape(v.shape[:-1] + (-1, 32))
    amax = np.abs(blocks).max(-1, keepdims=True)
    byte = np.maximum(np.where(amax > 0, np.frexp(amax)[1] - 1 + 127, 0) - down, 1)
    scale = np.exp2(byte - 127.0)
    codes = (blocks / scale).astype(np.float32).astype(dtype).astype(np.float64)
    return np.moveaxis((codes * scale).reshape(v.shape), -1, axis)


WIDE = False


def mx_kscale(k):
    if not WIDE:
        return np.ones(k)
    levels = np.array([10, -10, 5, -5, 0])
    if k % 512:
        return np.exp2(np.random.permutation(np.resize(levels, k // 32))).repeat(32)
    a = np.empty((k // 512, 16))
    for p in range(k // 512):
        a[p, :8] = np.random.permutation(np.resize(levels, 8))
        for g in range(8):
            far = levels[np.abs(levels - a[p, g]) >= 10]
            a[p, g + 8] = far[np.random.randint(len(far))]
    return np.exp2(a.ravel()).repeat(32)


def f64(x):
    return np.asarray(x).astype(np.float64)


E2M1 = np.array([0.0, 0.5, 1.0, 1.5, 2.0, 3.0, 4.0, 6.0, -0.0, -0.5, -1.0, -1.5, -2.0, -3.0, -4.0, -6.0])


def pack_weight(w, fmt):
    k, n = w.shape
    w = f64(np.asarray(w, np.float32).astype(ml_dtypes.bfloat16)).reshape(k // 32, 32, n)
    amax = np.abs(w).max(1)
    if fmt == "e4m3":
        byte = np.frexp(amax)[1] - 1 + 127 - 7
    else:
        mant, ex = np.frexp(amax / 6.0)
        byte = np.where(mant > 0.5, ex, ex - 1) + 127
    byte = np.clip(np.where(amax > 0, byte, 1), 1, 254)
    scaled = (w * np.exp2(127.0 - byte)[:, None, :]).reshape(k, n).astype(np.float32)
    by_word = np.ascontiguousarray(scaled.reshape(k // 512, 128, 4, n).transpose(0, 1, 3, 2))
    if fmt == "e4m3":
        words = by_word.astype(ml_dtypes.float8_e4m3fn).view(np.uint8)
    else:
        c = by_word.astype(ml_dtypes.float4_e2m1fn).view(np.uint8) & 0xF
        words = (c[..., 0::2] | (c[..., 1::2] << 4)).reshape(k // 512, 128, 2 * n)
    return np.ascontiguousarray(words), np.ascontiguousarray(byte.astype(np.uint8).reshape(k // 512, 16, n))


def unpack_weight(words, scales, fmt):
    g, _, n = scales.shape
    words = np.ascontiguousarray(words).reshape(g, 128, n, -1)
    if fmt == "e4m3":
        vals = words.view(ml_dtypes.float8_e4m3fn).astype(np.float64)
    else:
        nib = np.empty((g, 128, n, 4), np.uint8)
        nib[..., 0::2] = words & 0xF
        nib[..., 1::2] = words >> 4
        vals = E2M1[nib]
    vals = vals * np.repeat(np.exp2(scales.astype(np.float64) - 127.0), 8, axis=1)[..., None]
    return vals.transpose(0, 1, 3, 2).reshape(g * 512, n)


def sigmoid(v):
    return 1.0 / (1.0 + np.exp(-v))


def bf(x):
    return np.asarray(x, np.float32).astype(ml_dtypes.bfloat16)


def planes(Y):
    r, m = Y.shape
    b = f64(bf(Y)).reshape(r // 32, 32, m)
    amax = np.abs(b).max(1)
    byte = np.clip(np.where(amax > 0, np.frexp(amax)[1] - 1 + 127 - 7, 1), 1, 254)
    codes = (b * np.exp2(127.0 - byte)[:, None, :]).reshape(r, m).astype(np.float32).astype(ml_dtypes.float8_e4m3fn).view(np.uint8)
    words = codes.reshape(r // 512, 128, 4, m).transpose(0, 1, 3, 2)
    return np.ascontiguousarray(words), np.ascontiguousarray(byte.astype(np.uint8).reshape(r // 512, 16, m))


K, L, T, R, N = 1024, 512, 512, 512, 512


def setup_inputs():
    n = np.random.standard_normal
    fk = mx_kscale(K)
    fl = mx_kscale(L)
    fr = mx_kscale(R)
    xtp = pack_weight(n((K, T)) / fk[:, None], "e2m1")
    wap = pack_weight(n((K, R)) * 1 / np.sqrt(K) * fk[:, None], "e4m3")
    xqp = pack_weight(n((L, T)) / fl[:, None], "e2m1")
    wcp = pack_weight(n((L, R)) * 1 / np.sqrt(L) * fl[:, None], "e4m3")
    wgp = pack_weight(n((K, R)) * 1 / np.sqrt(K) * fk[:, None], "e2m1")
    wbp = pack_weight(n((R, N)) * 1 / np.sqrt(R) / fr[:, None], "e4m3")
    wyp = pack_weight(n((K, N)) * 1 / np.sqrt(K) * fk[:, None], "e4m3")
    return {
        "xt_words": xtp[0],
        "xt_scales": xtp[1],
        "wa_words": wap[0],
        "wa_scales": wap[1],
        "xq_words": xqp[0],
        "xq_scales": xqp[1],
        "wc_words": wcp[0],
        "wc_scales": wcp[1],
        "wg_words": wgp[0],
        "wg_scales": wgp[1],
        "us": (np.random.uniform(0.5, 2.0, (R, 1)) * fr[:, None]).astype(np.float32),
        "wb_words": wbp[0],
        "wb_scales": wbp[1],
        "wy_words": wyp[0],
        "wy_scales": wyp[1],
    }


def reference(xt_words, xt_scales, wa_words, wa_scales, xq_words, xq_scales, wc_words, wc_scales, wg_words, wg_scales, us, wb_words, wb_scales, wy_words, wy_scales):
    xtu = unpack_weight(xt_words, xt_scales, "e2m1")
    wau = unpack_weight(wa_words, wa_scales, "e4m3")
    xqu = unpack_weight(xq_words, xq_scales, "e2m1")
    wcu = unpack_weight(wc_words, wc_scales, "e4m3")
    wgu = unpack_weight(wg_words, wg_scales, "e2m1")
    wbu = unpack_weight(wb_words, wb_scales, "e4m3")
    wyu = unpack_weight(wy_words, wy_scales, "e4m3")
    a = wau.T @ xtu
    b = wcu.T @ xqu
    g = wgu.T @ xtu
    hid = (b + sigmoid(g) * (a - b)) * f64(us)
    hidq = mxq(hid, 0, "e4m3")
    y = wbu.T @ hidq + wyu.T @ xtu
    words, scales = planes(y)
    return y, words, scales

@@ -1,0 +1,254 @@
+from contextlib import ExitStack
+
+import concourse.mybir as mybir
+from concourse.masks import make_identity
+
+F32 = mybir.dt.float32
+BF16 = mybir.dt.bfloat16
+I32 = mybir.dt.int32
+U8 = mybir.dt.uint8
+FP8X4 = mybir.dt.float8_e4m3fn_x4
+FP4X4 = mybir.dt.float4_e2m1fn_x4
+ACT = mybir.ActivationFunctionType
+ALU = mybir.AluOpType
+
+K, L, T, R, N = 1024, 512, 512, 512, 512
+P = 128
+PACK = 4
+WIDE = 512
+TILES = T // P
+FLOPS = 2 * T * (K * R + L * R + K * R + R * N + K * N)
+
+
+def tile_mix_hidden_chosen_by_gate_pl_kernel(
+    tc, xt_words, xt_scales, wa_words, wa_scales, xq_words, xq_scales, wc_words, wc_scales,
+    wg_words, wg_scales, us, wb_words, wb_scales, wy_words, wy_scales, out_0, out_1, out_2,
+):
+    nc = tc.nc
+    with ExitStack() as ctx:
+        keep = ctx.enter_context(tc.tile_pool(name="keep", bufs=1))
+        work = ctx.enter_context(tc.tile_pool(name="work", bufs=2))
+        psum = ctx.enter_context(tc.psum_pool(name="psum", bufs=1))
+        ctx.enter_context(tc.manual_schedule())
+
+        first_scales = [xt_scales, wg_scales, wa_scales, xq_scales, wc_scales]
+        second_scales = [wy_scales, wb_scales]
+        first_stage = keep.tile([P, 8, WIDE // 4], I32)
+        second_stage = keep.tile([P, 3, WIDE], U8, align_bytes=64)
+        first_planes = keep.tile([P, 8, WIDE], U8, align_bytes=64)
+        second_dealt = keep.tile([P, 3, WIDE], U8, align_bytes=64)
+        second_planes = keep.tile([P, 3, WIDE], U8, align_bytes=64)
+        xt = keep.tile([P, 2, 2 * T], U8, align_bytes=64)
+        wg = keep.tile([P, 2, 2 * R], U8, align_bytes=64)
+        xq = keep.tile([P, 1, 2 * T], U8, align_bytes=64)
+        wa = keep.tile([P, 2, R], I32, align_bytes=64)
+        wc = keep.tile([P, 1, R], I32, align_bytes=64)
+        wy_raw = keep.tile([P, 2, N], I32, align_bytes=64)
+        wb_raw = keep.tile([P, 1, N], I32, align_bytes=64)
+        second_words = keep.tile([P, 3, N], I32, align_bytes=64)
+        us_sb = keep.tile([P, PACK], F32)
+        ident = keep.tile([P, P], F32)
+        y_codes = keep.tile([P, T], I32, align_bytes=64)
+        y_scales = keep.tile([P, T], U8, align_bytes=64)
+
+        def stage_scales(queue, stage, tensors, at):
+            for scales in tensors:
+                passes = scales.shape[0]
+                queue.dma_start(out=stage[0:P:8, at:at + passes, :], in_=scales.rearrange("z q c -> q z c").bitcast(I32))
+                at = at + passes
+
+        def place_scales(queue, planes, stage):
+            for q in range(4):
+                queue.dma_start(out=planes[32 * q:32 * q + 4, :, :].bitcast(I32), in_=stage[32 * q:32 * q + 32:8, :, :])
+
+        def load_fp4(queue, tile, words):
+            queue.dma_start(out=tile[:].bitcast(I32), in_=words.rearrange("z p c -> p z c").bitcast(I32))
+
+        def load_fp8(queue, tile, words):
+            queue.dma_start(out=tile[:], in_=words.rearrange("z p c r -> p z (c r)").bitcast(I32))
+
+        def deal_scales():
+            nc.vector.tensor_copy(
+                out=second_dealt[:].rearrange("p z (i c e) -> p z c i e", i=PACK, e=16),
+                in_=second_stage[:].rearrange("p z (c e i) -> p z c i e", i=PACK, e=16),
+            )
+
+        stage_scales(nc.sync, first_stage[:], first_scales[:3], 0)
+        stage_scales(nc.scalar, first_stage[:], first_scales[3:], 6)
+        load_fp4(nc.scalar, xt, xt_words)
+        load_fp4(nc.scalar, wg, wg_words)
+        load_fp8(nc.scalar, wa, wa_words)
+        nc.vector.memset(second_stage[:].bitcast(I32), 0)
+        nc.vector.memset(first_planes[:].bitcast(I32), 0)
+        nc.vector.memset(second_planes[:].bitcast(I32), 0)
+        stage_scales(nc.gpsimd, second_stage[:].bitcast(I32), second_scales, 0)
+        nc.gpsimd.dma_start(out=us_sb[:], in_=us.rearrange("(p j) o -> p (j o)", j=PACK))
+        make_identity(nc, ident[:])
+        place_scales(nc.sync, first_planes, first_stage[:])
+        load_fp4(nc.sync, xq, xq_words)
+        load_fp8(nc.sync, wc, wc_words)
+        load_fp8(nc.sync, wy_raw, wy_words)
+        load_fp8(nc.sync, wb_raw, wb_words)
+        deal_scales()
+        place_scales(nc.sync, second_planes, second_dealt[:].bitcast(I32))
+
+        XT, WG, WA, XQ, WC = 0, 2, 4, 6, 7
+        banks = {}
+        tiles = {}
+
+        def first_product(name, tag, bufs, tt, x, x_at, w, w_at, w_dtype):
+            bank = psum.tile([P, WIDE], F32, tag=tag, name=name, bufs=bufs)
+            passes = x.shape[1]
+            for z in range(passes):
+                nc.tensor.matmul_mx(
+                    out=bank[:],
+                    lhsT=x[:, z, 2 * P * tt:2 * P * (tt + 1)].bitcast(FP4X4),
+                    lhsT_scale=first_planes[:, x_at + z, P * tt:P * (tt + 1)],
+                    rhs=w[:, z, :].bitcast(w_dtype),
+                    rhs_scale=first_planes[:, w_at + z, :],
+                    start=(z == 0), stop=(z == passes - 1),
+                )
+            banks[name, tt] = bank
+
+        def first_layer(tt):
+            first_product("g", "g", 2, tt, xt, XT, wg, WG, FP4X4)
+            first_product("a", "ab", 3, tt, xt, XT, wa, WA, FP8X4)
+            first_product("b", "ab", 3, tt, xq, XQ, wc, WC, FP8X4)
+
+        def dealt(bank):
+            return bank[:].rearrange("t (m j) -> t j m", j=PACK)
+
+        def gates(tt):
+            for name, sign in (("a", 1.0), ("b", -1.0)):
+                gate = work.tile([P, PACK, P], F32, tag="gate_" + name, name="gate_" + name)
+                nc.scalar.activation(out=gate[:], in_=dealt(banks["g", tt]), func=ACT.Sigmoid, scale=sign)
+                tiles["gate", name, tt] = gate
+
+        def products(tt):
+            for name in ("a", "b"):
+                part = work.tile([P, PACK, P], F32, tag="part_" + name, name="part_" + name)
+                nc.vector.tensor_tensor(out=part[:], in0=dealt(banks[name, tt]), in1=tiles["gate", name, tt][:], op=ALU.mult)
+                tiles["part", name, tt] = part
+
+        def turn(tt):
+            mix = psum.tile([P, PACK, P], F32, tag="mix", name="mix", bufs=1)
+            for name in ("a", "b"):
+                for j in range(PACK):
+                    nc.tensor.matmul(
+                        out=mix[:, j, :], lhsT=tiles["part", name, tt][:, j, :], rhs=ident[:], is_transpose=True,
+                        start=(name == "a" and j == 0), stop=(name == "b" and j == PACK - 1),
+                    )
+            banks["mix", tt] = mix
+
+        def round_hid(tt):
+            hid = work.tile([P, P, PACK], BF16, tag="hid", name="hid", align_bytes=64)
+            nc.vector.tensor_tensor(
+                out=hid[:], in0=banks["mix", tt][:].rearrange("p j t -> p t j"),
+                in1=us_sb[:].unsqueeze(1).to_broadcast([P, P, PACK]), op=ALU.mult,
+            )
+            tiles["hid", tt] = hid
+
+        def quantise_hid(tt):
+            codes = work.tile([P, P], I32, tag="hid_codes", name="hid_codes", align_bytes=64, bufs=4)
+            scales = work.tile([P, P], U8, tag="hid_scales", name="hid_scales", align_bytes=64, bufs=4)
+            nc.vector.quantize_mx(out=codes[:].bitcast(FP8X4), scales=scales[:], in_=tiles["hid", tt][:].rearrange("p t j -> p (t j)"))
+            tiles["hid_codes", tt] = codes
+            tiles["hid_scales", tt] = scales
+
+        def deal_words(at, raw, z):
+            nc.vector.tensor_copy(
+                out=second_words[:, at, :].rearrange("p (i c e) -> p c i e", i=PACK, e=4),
+                in_=raw[:, z, :].rearrange("p (c e i) -> p c i e", i=PACK, e=4),
+            )
+
+        def second_layer(tt):
+            y = psum.tile([P, PACK, P], F32, tag="y", name="y", bufs=2)
+            cols = slice(P * tt, P * (tt + 1))
+            for z in range(3):
+                for i in range(PACK):
+                    rows = slice(P * i, P * (i + 1))
+                    if z < 2:
+                        rhs = xt[:, z, 2 * P * tt:2 * P * (tt + 1)].bitcast(FP4X4)
+                        rhs_scale = first_planes[:, XT + z, cols]
+                    else:
+                        rhs = tiles["hid_codes", tt][:].bitcast(FP8X4)
+                        rhs_scale = tiles["hid_scales", tt][:]
+                    nc.tensor.matmul_mx(
+                        out=y[:, i, :], lhsT=second_words[:, z, rows].bitcast(FP8X4), lhsT_scale=second_planes[:, z, rows],
+                        rhs=rhs, rhs_scale=rhs_scale, start=(z == 0 and i == 0), stop=(z == 2 and i == PACK - 1),
+                    )
+            banks["y", tt] = y
+
+        out_rows = out_0.rearrange("(p i) t -> p i t", i=PACK)
+
+        def store_y(tt):
+            y_sb = work.tile([P, PACK, P], F32, tag="y_sb", name="y_sb", bufs=4)
+            nc.scalar.copy(out=y_sb[:], in_=banks["y", tt][:])
+            nc.sync.dma_start(out=out_rows[:, :, P * tt:P * (tt + 1)], in_=y_sb[:])
+            tiles["y_sb", tt] = y_sb
+
+        def round_y(tt, from_psum):
+            y_bf = work.tile([P, P, PACK], BF16, tag="y_bf", name="y_bf", align_bytes=64)
+            if from_psum:
+                nc.scalar.copy(out=y_bf[:], in_=banks["y", tt][:].rearrange("p i t -> p t i"))
+            else:
+                nc.vector.tensor_copy(
+                    out=y_bf[:].rearrange("p (c e) i -> p c i e", e=4),
+                    in_=tiles["y_sb", tt][:].rearrange("p i (c e) -> p c i e", e=4),
+                )
+            tiles["y_bf", tt] = y_bf
+
+        def quantise_y(tt):
+            cols = slice(P * tt, P * (tt + 1))
+            nc.vector.quantize_mx(out=y_codes[:, cols].bitcast(FP8X4), scales=y_scales[:, cols], in_=tiles["y_bf", tt][:].rearrange("p t i -> p (t i)"))
+
+        codes_out = out_1[0].rearrange("p c r -> p (c r)").bitcast(I32)
+
+        first_layer(0)
+        gates(0)
+        products(0)
+        first_layer(1)
+        gates(1)
+        deal_words(0, wy_raw, 0)
+        products(1)
+        turn(0)
+        first_layer(2)
+        gates(2)
+        round_hid(0)
+        deal_words(1, wy_raw, 1)
+        quantise_hid(0)
+        products(2)
+        turn(1)
+        round_hid(1)
+        deal_words(2, wb_raw, 0)
+        first_layer(3)
+        gates(3)
+        quantise_hid(1)
+        second_layer(0)
+        store_y(0)
+        products(3)
+        turn(2)
+        round_hid(2)
+        round_y(0, True)
+        second_layer(1)
+        quantise_y(0)
+        quantise_hid(2)
+        store_y(1)
+        round_y(1, True)
+        turn(3)
+        round_hid(3)
+        quantise_y(1)
+        quantise_hid(3)
+        nc.sync.dma_start(out=codes_out[:, 0:2 * P], in_=y_codes[:, 0:2 * P])
+        second_layer(2)
+        store_y(2)
+        round_y(2, False)
+        second_layer(3)
+        store_y(3)
+        quantise_y(2)
+        round_y(3, False)
+        quantise_y(3)
+        nc.sync.dma_start(out=codes_out[:, 2 * P:4 * P], in_=y_codes[:, 2 * P:4 * P])
+        for q in range(4):
+            queue = nc.scalar if q % 2 else nc.sync
+            queue.dma_start(out=out_2[0, 4 * q:4 * q + 4, :].bitcast(I32), in_=y_scales[32 * q:32 * q + 4, :].bitcast(I32))

@@ -17,6 +17,7 @@ P = 128
 PACK = 4
 WIDE = 512
 TILES = T // P
+WARM_PASSES = 18
 FLOPS = 2 * T * (K * R + L * R + K * R + R * N + K * N)
 
 
@@ -31,13 +32,14 @@ def tile_mix_hidden_chosen_by_gate_pl_kernel(
         psum = ctx.enter_context(tc.psum_pool(name="psum", bufs=1))
         ctx.enter_context(tc.manual_schedule())
 
-        first_scales = [xt_scales, wg_scales, wa_scales, xq_scales, wc_scales]
-        second_scales = [wy_scales, wb_scales]
-        first_stage = keep.tile([P, 8, WIDE // 4], I32)
+        gate_stage = keep.tile([P, 4, WIDE // 4], I32)
+        gate_planes = keep.tile([P, 4, WIDE], U8, align_bytes=64)
+        mix_planes = keep.tile([P, 4, WIDE], U8, align_bytes=64)
         second_stage = keep.tile([P, 3, WIDE], U8, align_bytes=64)
-        first_planes = keep.tile([P, 8, WIDE], U8, align_bytes=64)
-        second_dealt = keep.tile([P, 3, WIDE], U8, align_bytes=64)
         second_planes = keep.tile([P, 3, WIDE], U8, align_bytes=64)
+        warm_in = keep.tile([P, 4 * P], BF16, align_bytes=64)
+        warm_codes = keep.tile([P, P], I32, align_bytes=64)
+        warm_scales = keep.tile([P, P], U8, align_bytes=64)
         xt = keep.tile([P, 2, 2 * T], U8, align_bytes=64)
         wg = keep.tile([P, 2, 2 * R], U8, align_bytes=64)
         xq = keep.tile([P, 1, 2 * T], U8, align_bytes=64)
@@ -51,15 +53,16 @@ def tile_mix_hidden_chosen_by_gate_pl_kernel(
         y_codes = keep.tile([P, T], I32, align_bytes=64)
         y_scales = keep.tile([P, T], U8, align_bytes=64)
 
-        def stage_scales(queue, stage, tensors, at):
+        def stage_scales(queue, rows, tensors):
+            at = 0
             for scales in tensors:
                 passes = scales.shape[0]
-                queue.dma_start(out=stage[0:P:8, at:at + passes, :], in_=scales.rearrange("z q c -> q z c").bitcast(I32))
+                queue.dma_start(out=rows[:, at:at + passes, :], in_=scales.rearrange("z q c -> q z c").bitcast(I32))
                 at = at + passes
 
-        def place_scales(queue, planes, stage):
-            for q in range(4):
-                queue.dma_start(out=planes[32 * q:32 * q + 4, :, :].bitcast(I32), in_=stage[32 * q:32 * q + 32:8, :, :])
+        def place_scales(planes, rows, first):
+            for q in range(first, 4):
+                nc.sync.dma_start(out=planes[32 * q:32 * q + 4, :, :].bitcast(I32), in_=rows[4 * q:4 * q + 4, :, :])
 
         def load_fp4(queue, tile, words):
             queue.dma_start(out=tile[:].bitcast(I32), in_=words.rearrange("z p c -> p z c").bitcast(I32))
@@ -69,66 +72,83 @@ def tile_mix_hidden_chosen_by_gate_pl_kernel(
 
         def deal_scales():
             nc.vector.tensor_copy(
-                out=second_dealt[:].rearrange("p z (i c e) -> p z c i e", i=PACK, e=16),
+                out=second_planes[:].rearrange("p z (i c e) -> p z c i e", i=PACK, e=16),
                 in_=second_stage[:].rearrange("p z (c e i) -> p z c i e", i=PACK, e=16),
             )
 
-        stage_scales(nc.sync, first_stage[:], first_scales[:3], 0)
-        stage_scales(nc.scalar, first_stage[:], first_scales[3:], 6)
+        stage_scales(nc.sync, gate_stage[0:16], [xt_scales, wg_scales])
+        nc.vector.memset(mix_planes[:].bitcast(I32), 0)
+        stage_scales(nc.scalar, mix_planes[0:16].bitcast(I32), [wa_scales, xq_scales, wc_scales])
         load_fp4(nc.scalar, xt, xt_words)
         load_fp4(nc.scalar, wg, wg_words)
         load_fp8(nc.scalar, wa, wa_words)
-        nc.vector.memset(second_stage[:].bitcast(I32), 0)
-        nc.vector.memset(first_planes[:].bitcast(I32), 0)
-        nc.vector.memset(second_planes[:].bitcast(I32), 0)
-        stage_scales(nc.gpsimd, second_stage[:].bitcast(I32), second_scales, 0)
+        nc.vector.memset(warm_in[:].bitcast(I32), 0)
+        nc.vector.memset(gate_planes[:].bitcast(I32), 0)
+        nc.vector.quantize_mx(out=warm_codes[:].bitcast(FP8X4), scales=warm_scales[:], in_=warm_in[:])
+        warm = psum.tile([P, PACK, P], F32, tag="mix", name="warm", bufs=1)
+        for i in range(WARM_PASSES):
+            nc.tensor.matmul_mx(
+                out=warm[:, i % PACK, :], lhsT=warm_codes[:].bitcast(FP8X4), lhsT_scale=warm_scales[:],
+                rhs=warm_codes[:].bitcast(FP8X4), rhs_scale=warm_scales[:], start=True, stop=True,
+            )
+        nc.gpsimd.memset(second_stage[:].bitcast(I32), 0)
+        stage_scales(nc.gpsimd, second_stage[0:16].bitcast(I32), [wy_scales, wb_scales])
         nc.gpsimd.dma_start(out=us_sb[:], in_=us.rearrange("(p j) o -> p (j o)", j=PACK))
         make_identity(nc, ident[:])
-        place_scales(nc.sync, first_planes, first_stage[:])
+        place_scales(gate_planes, gate_stage, 0)
+        place_scales(mix_planes, mix_planes[:].bitcast(I32), 1)
         load_fp4(nc.sync, xq, xq_words)
         load_fp8(nc.sync, wc, wc_words)
         load_fp8(nc.sync, wy_raw, wy_words)
         load_fp8(nc.sync, wb_raw, wb_words)
         deal_scales()
-        place_scales(nc.sync, second_planes, second_dealt[:].bitcast(I32))
+        place_scales(second_planes, second_planes[:].bitcast(I32), 1)
 
-        XT, WG, WA, XQ, WC = 0, 2, 4, 6, 7
         banks = {}
         tiles = {}
 
-        def first_product(name, tag, bufs, tt, x, x_at, w, w_at, w_dtype):
+        first = {
+            "g": (xt, gate_planes, 0, wg, gate_planes, 2, FP4X4, "g", 2),
+            "a": (xt, gate_planes, 0, wa, mix_planes, 0, FP8X4, "ab", 3),
+            "b": (xq, mix_planes, 2, wc, mix_planes, 3, FP8X4, "ab", 3),
+        }
+
+        def first_product(name, tt):
+            x, x_planes, x_at, w, w_planes, w_at, w_dtype, tag, bufs = first[name]
             bank = psum.tile([P, WIDE], F32, tag=tag, name=name, bufs=bufs)
             passes = x.shape[1]
             for z in range(passes):
                 nc.tensor.matmul_mx(
                     out=bank[:],
                     lhsT=x[:, z, 2 * P * tt:2 * P * (tt + 1)].bitcast(FP4X4),
-                    lhsT_scale=first_planes[:, x_at + z, P * tt:P * (tt + 1)],
+                    lhsT_scale=x_planes[:, x_at + z, P * tt:P * (tt + 1)],
                     rhs=w[:, z, :].bitcast(w_dtype),
-                    rhs_scale=first_planes[:, w_at + z, :],
+                    rhs_scale=w_planes[:, w_at + z, :],
                     start=(z == 0), stop=(z == passes - 1),
                 )
             banks[name, tt] = bank
 
-        def first_layer(tt):
-            first_product("g", "g", 2, tt, xt, XT, wg, WG, FP4X4)
-            first_product("a", "ab", 3, tt, xt, XT, wa, WA, FP8X4)
-            first_product("b", "ab", 3, tt, xq, XQ, wc, WC, FP8X4)
+        def dealt_read(bank):
+            return bank[:].rearrange("t (c e j) -> t c j e", j=PACK, e=4)
 
-        def dealt(bank):
-            return bank[:].rearrange("t (m j) -> t j m", j=PACK)
+        def dealt(tile):
+            return tile[:].rearrange("t j (c e) -> t c j e", e=4)
 
         def gates(tt):
+            first_product("g", tt)
             for name, sign in (("a", 1.0), ("b", -1.0)):
-                gate = work.tile([P, PACK, P], F32, tag="gate_" + name, name="gate_" + name)
-                nc.scalar.activation(out=gate[:], in_=dealt(banks["g", tt]), func=ACT.Sigmoid, scale=sign)
+                gate = work.tile([P, PACK, P], F32, tag="gate_" + name, name="gate_" + name, bufs=3)
+                nc.scalar.activation(out=dealt(gate), in_=dealt_read(banks["g", tt]), func=ACT.Sigmoid, scale=sign)
                 tiles["gate", name, tt] = gate
 
+        def product(name, tt):
+            part = work.tile([P, PACK, P], F32, tag="part_" + name, name="part_" + name)
+            nc.vector.tensor_tensor(out=dealt(part), in0=dealt_read(banks[name, tt]), in1=dealt(tiles["gate", name, tt]), op=ALU.mult)
+            tiles["part", name, tt] = part
+
         def products(tt):
-            for name in ("a", "b"):
-                part = work.tile([P, PACK, P], F32, tag="part_" + name, name="part_" + name)
-                nc.vector.tensor_tensor(out=part[:], in0=dealt(banks[name, tt]), in1=tiles["gate", name, tt][:], op=ALU.mult)
-                tiles["part", name, tt] = part
+            product("a", tt)
+            product("b", tt)
 
         def turn(tt):
             mix = psum.tile([P, PACK, P], F32, tag="mix", name="mix", bufs=1)
@@ -169,7 +189,7 @@ def tile_mix_hidden_chosen_by_gate_pl_kernel(
                     rows = slice(P * i, P * (i + 1))
                     if z < 2:
                         rhs = xt[:, z, 2 * P * tt:2 * P * (tt + 1)].bitcast(FP4X4)
-                        rhs_scale = first_planes[:, XT + z, cols]
+                        rhs_scale = gate_planes[:, z, cols]
                     else:
                         rhs = tiles["hid_codes", tt][:].bitcast(FP8X4)
                         rhs_scale = tiles["hid_scales", tt][:]
@@ -192,10 +212,7 @@ def tile_mix_hidden_chosen_by_gate_pl_kernel(
             if from_psum:
                 nc.scalar.copy(out=y_bf[:], in_=banks["y", tt][:].rearrange("p i t -> p t i"))
             else:
-                nc.vector.tensor_copy(
-                    out=y_bf[:].rearrange("p (c e) i -> p c i e", e=4),
-                    in_=tiles["y_sb", tt][:].rearrange("p i (c e) -> p c i e", e=4),
-                )
+                nc.vector.tensor_copy(out=y_bf[:], in_=tiles["y_sb", tt][:].rearrange("p i t -> p t i"))
             tiles["y_bf", tt] = y_bf
 
         def quantise_y(tt):
@@ -204,25 +221,30 @@ def tile_mix_hidden_chosen_by_gate_pl_kernel(
 
         codes_out = out_1[0].rearrange("p c r -> p (c r)").bitcast(I32)
 
-        first_layer(0)
         gates(0)
-        products(0)
-        first_layer(1)
         gates(1)
-        deal_words(0, wy_raw, 0)
+        first_product("a", 0)
+        first_product("a", 1)
+        product("a", 0)
+        first_product("b", 0)
+        gates(2)
+        product("b", 0)
+        first_product("b", 1)
         products(1)
         turn(0)
-        first_layer(2)
-        gates(2)
+        first_product("a", 2)
+        first_product("b", 2)
         round_hid(0)
-        deal_words(1, wy_raw, 1)
+        deal_words(0, wy_raw, 0)
         quantise_hid(0)
-        products(2)
+        gates(3)
         turn(1)
+        deal_words(1, wy_raw, 1)
+        products(2)
+        first_product("a", 3)
+        first_product("b", 3)
         round_hid(1)
         deal_words(2, wb_raw, 0)
-        first_layer(3)
-        gates(3)
         quantise_hid(1)
         second_layer(0)
         store_y(0)

@@ -17,7 +17,7 @@ P = 128
 PACK = 4
 WIDE = 512
 TILES = T // P
-WARM_PASSES = 18
+WARM_PASSES = 24
 FLOPS = 2 * T * (K * R + L * R + K * R + R * N + K * N)
 
 
@@ -60,8 +60,8 @@ def tile_mix_hidden_chosen_by_gate_pl_kernel(
                 queue.dma_start(out=rows[:, at:at + passes, :], in_=scales.rearrange("z q c -> q z c").bitcast(I32))
                 at = at + passes
 
-        def place_scales(planes, rows, first):
-            for q in range(first, 4):
+        def place_scales(planes, rows, quadrants):
+            for q in quadrants:
                 nc.sync.dma_start(out=planes[32 * q:32 * q + 4, :, :].bitcast(I32), in_=rows[4 * q:4 * q + 4, :, :])
 
         def load_fp4(queue, tile, words):
@@ -79,9 +79,9 @@ def tile_mix_hidden_chosen_by_gate_pl_kernel(
         stage_scales(nc.sync, gate_stage[0:16], [xt_scales, wg_scales])
         nc.vector.memset(mix_planes[:].bitcast(I32), 0)
         stage_scales(nc.scalar, mix_planes[0:16].bitcast(I32), [wa_scales, xq_scales, wc_scales])
-        load_fp4(nc.scalar, xt, xt_words)
-        load_fp4(nc.scalar, wg, wg_words)
-        load_fp8(nc.scalar, wa, wa_words)
+        load_fp4(nc.sync, xt, xt_words)
+        load_fp4(nc.sync, wg, wg_words)
+        load_fp4(nc.sync, xq, xq_words)
         nc.vector.memset(warm_in[:].bitcast(I32), 0)
         nc.vector.memset(gate_planes[:].bitcast(I32), 0)
         nc.vector.quantize_mx(out=warm_codes[:].bitcast(FP8X4), scales=warm_scales[:], in_=warm_in[:])
@@ -93,16 +93,17 @@ def tile_mix_hidden_chosen_by_gate_pl_kernel(
             )
         nc.gpsimd.memset(second_stage[:].bitcast(I32), 0)
         stage_scales(nc.gpsimd, second_stage[0:16].bitcast(I32), [wy_scales, wb_scales])
-        nc.gpsimd.dma_start(out=us_sb[:], in_=us.rearrange("(p j) o -> p (j o)", j=PACK))
         make_identity(nc, ident[:])
-        place_scales(gate_planes, gate_stage, 0)
-        place_scales(mix_planes, mix_planes[:].bitcast(I32), 1)
-        load_fp4(nc.sync, xq, xq_words)
+        nc.gpsimd.dma_start(out=us_sb[:], in_=us.rearrange("(p j) o -> p (j o)", j=PACK))
+        place_scales(gate_planes, gate_stage, [0])
         load_fp8(nc.sync, wc, wc_words)
+        place_scales(gate_planes, gate_stage, [1, 2, 3])
+        place_scales(mix_planes, mix_planes[:].bitcast(I32), [1, 2, 3])
+        load_fp8(nc.sync, wa, wa_words)
         load_fp8(nc.sync, wy_raw, wy_words)
         load_fp8(nc.sync, wb_raw, wb_words)
         deal_scales()
-        place_scales(second_planes, second_planes[:].bitcast(I32), 1)
+        place_scales(second_planes, second_planes[:].bitcast(I32), [1, 2, 3])
 
         banks = {}
         tiles = {}
@@ -136,7 +137,7 @@ def tile_mix_hidden_chosen_by_gate_pl_kernel(
 
         def gates(tt):
             first_product("g", tt)
-            for name, sign in (("a", 1.0), ("b", -1.0)):
+            for name, sign in (("b", -1.0), ("a", 1.0)):
                 gate = work.tile([P, PACK, P], F32, tag="gate_" + name, name="gate_" + name, bufs=3)
                 nc.scalar.activation(out=dealt(gate), in_=dealt_read(banks["g", tt]), func=ACT.Sigmoid, scale=sign)
                 tiles["gate", name, tt] = gate
@@ -147,16 +148,16 @@ def tile_mix_hidden_chosen_by_gate_pl_kernel(
             tiles["part", name, tt] = part
 
         def products(tt):
-            product("a", tt)
             product("b", tt)
+            product("a", tt)
 
         def turn(tt):
             mix = psum.tile([P, PACK, P], F32, tag="mix", name="mix", bufs=1)
-            for name in ("a", "b"):
+            for name in ("b", "a"):
                 for j in range(PACK):
                     nc.tensor.matmul(
                         out=mix[:, j, :], lhsT=tiles["part", name, tt][:, j, :], rhs=ident[:], is_transpose=True,
-                        start=(name == "a" and j == 0), stop=(name == "b" and j == PACK - 1),
+                        start=(name == "b" and j == 0), stop=(name == "a" and j == PACK - 1),
                     )
             banks["mix", tt] = mix
 
@@ -223,17 +224,17 @@ def tile_mix_hidden_chosen_by_gate_pl_kernel(
 
         gates(0)
         gates(1)
-        first_product("a", 0)
-        first_product("a", 1)
-        product("a", 0)
         first_product("b", 0)
-        gates(2)
-        product("b", 0)
         first_product("b", 1)
+        product("b", 0)
+        first_product("a", 0)
+        gates(2)
+        product("a", 0)
+        first_product("a", 1)
         products(1)
         turn(0)
-        first_product("a", 2)
         first_product("b", 2)
+        first_product("a", 2)
         round_hid(0)
         deal_words(0, wy_raw, 0)
         quantise_hid(0)
@@ -241,8 +242,8 @@ def tile_mix_hidden_chosen_by_gate_pl_kernel(
         turn(1)
         deal_words(1, wy_raw, 1)
         products(2)
-        first_product("a", 3)
         first_product("b", 3)
+        first_product("a", 3)
         round_hid(1)
         deal_words(2, wb_raw, 0)
         quantise_hid(1)

@@ -13,12 +13,19 @@ ACT = mybir.ActivationFunctionType
 ALU = mybir.AluOpType
 
 K, L, T, R, N = 1024, 512, 512, 512, 512
+FLOPS = 2 * T * (K * R + L * R + K * R + R * N + K * N)
+
 P = 128
 PACK = 4
 WIDE = 512
 TILES = T // P
-WARM_PASSES = 24
-FLOPS = 2 * T * (K * R + L * R + K * R + R * N + K * N)
+SCALE_ROWS = 16
+QUADRANTS = 4
+LINE_WORDS = 4
+LINE_BYTES = 16
+WARM_PASSES = 20
+PRODUCT_BANKS = 3
+PART_TILES = 3
 
 
 def tile_mix_hidden_chosen_by_gate_pl_kernel(
@@ -34,10 +41,10 @@ def tile_mix_hidden_chosen_by_gate_pl_kernel(
 
         gate_stage = keep.tile([P, 4, WIDE // 4], I32)
         gate_planes = keep.tile([P, 4, WIDE], U8, align_bytes=64)
-        mix_planes = keep.tile([P, 4, WIDE], U8, align_bytes=64)
+        value_planes = keep.tile([P, 4, WIDE], U8, align_bytes=64)
         second_stage = keep.tile([P, 3, WIDE], U8, align_bytes=64)
         second_planes = keep.tile([P, 3, WIDE], U8, align_bytes=64)
-        warm_in = keep.tile([P, 4 * P], BF16, align_bytes=64)
+        warm_in = keep.tile([P, PACK * P], BF16, align_bytes=64)
         warm_codes = keep.tile([P, P], I32, align_bytes=64)
         warm_scales = keep.tile([P, P], U8, align_bytes=64)
         xt = keep.tile([P, 2, 2 * T], U8, align_bytes=64)
@@ -64,24 +71,31 @@ def tile_mix_hidden_chosen_by_gate_pl_kernel(
             for q in quadrants:
                 nc.sync.dma_start(out=planes[32 * q:32 * q + 4, :, :].bitcast(I32), in_=rows[4 * q:4 * q + 4, :, :])
 
-        def load_fp4(queue, tile, words):
-            queue.dma_start(out=tile[:].bitcast(I32), in_=words.rearrange("z p c -> p z c").bitcast(I32))
+        def load_fp4(tile, words):
+            nc.sync.dma_start(out=tile[:].bitcast(I32), in_=words.rearrange("z p c -> p z c").bitcast(I32))
 
-        def load_fp8(queue, tile, words):
-            queue.dma_start(out=tile[:], in_=words.rearrange("z p c r -> p z (c r)").bitcast(I32))
+        def load_fp8(tile, words):
+            nc.sync.dma_start(out=tile[:], in_=words.rearrange("z p c r -> p z (c r)").bitcast(I32))
 
-        def deal_scales():
+        def deal_scales(passes):
             nc.vector.tensor_copy(
-                out=second_planes[:].rearrange("p z (i c e) -> p z c i e", i=PACK, e=16),
-                in_=second_stage[:].rearrange("p z (c e i) -> p z c i e", i=PACK, e=16),
+                out=second_planes[:, passes, :].rearrange("p z (i c e) -> p z c i e", i=PACK, e=LINE_BYTES),
+                in_=second_stage[:, passes, :].rearrange("p z (c e i) -> p z c i e", i=PACK, e=LINE_BYTES),
             )
 
-        stage_scales(nc.sync, gate_stage[0:16], [xt_scales, wg_scales])
-        nc.vector.memset(mix_planes[:].bitcast(I32), 0)
-        stage_scales(nc.scalar, mix_planes[0:16].bitcast(I32), [wa_scales, xq_scales, wc_scales])
-        load_fp4(nc.sync, xt, xt_words)
-        load_fp4(nc.sync, wg, wg_words)
-        load_fp4(nc.sync, xq, xq_words)
+        def deal_words(at, raw, z):
+            nc.vector.tensor_copy(
+                out=second_words[:, at, :].rearrange("p (i c e) -> p c i e", i=PACK, e=LINE_WORDS),
+                in_=raw[:, z, :].rearrange("p (c e i) -> p c i e", i=PACK, e=LINE_WORDS),
+            )
+
+        stage_scales(nc.sync, gate_stage[0:SCALE_ROWS], [xt_scales, wg_scales])
+        nc.vector.memset(value_planes[:].bitcast(I32), 0)
+        stage_scales(nc.sync, value_planes[0:SCALE_ROWS].bitcast(I32), [wa_scales, xq_scales, wc_scales])
+        load_fp4(xt, xt_words)
+        load_fp4(wg, wg_words)
+        load_fp4(xq, xq_words)
+
         nc.vector.memset(warm_in[:].bitcast(I32), 0)
         nc.vector.memset(gate_planes[:].bitcast(I32), 0)
         nc.vector.quantize_mx(out=warm_codes[:].bitcast(FP8X4), scales=warm_scales[:], in_=warm_in[:])
@@ -91,31 +105,32 @@ def tile_mix_hidden_chosen_by_gate_pl_kernel(
                 out=warm[:, i % PACK, :], lhsT=warm_codes[:].bitcast(FP8X4), lhsT_scale=warm_scales[:],
                 rhs=warm_codes[:].bitcast(FP8X4), rhs_scale=warm_scales[:], start=True, stop=True,
             )
+
         nc.gpsimd.memset(second_stage[:].bitcast(I32), 0)
-        stage_scales(nc.gpsimd, second_stage[0:16].bitcast(I32), [wy_scales, wb_scales])
+        stage_scales(nc.gpsimd, second_stage[0:SCALE_ROWS].bitcast(I32), [wy_scales, wb_scales])
         make_identity(nc, ident[:])
         nc.gpsimd.dma_start(out=us_sb[:], in_=us.rearrange("(p j) o -> p (j o)", j=PACK))
-        place_scales(gate_planes, gate_stage, [0])
-        load_fp8(nc.sync, wc, wc_words)
-        place_scales(gate_planes, gate_stage, [1, 2, 3])
-        place_scales(mix_planes, mix_planes[:].bitcast(I32), [1, 2, 3])
-        load_fp8(nc.sync, wa, wa_words)
-        load_fp8(nc.sync, wy_raw, wy_words)
-        load_fp8(nc.sync, wb_raw, wb_words)
-        deal_scales()
-        place_scales(second_planes, second_planes[:].bitcast(I32), [1, 2, 3])
+
+        place_scales(gate_planes, gate_stage, range(QUADRANTS))
+        load_fp8(wc, wc_words)
+        place_scales(value_planes, value_planes[:].bitcast(I32), range(1, QUADRANTS))
+        load_fp8(wa, wa_words)
+        load_fp8(wy_raw, wy_words)
+        load_fp8(wb_raw, wb_words)
+        deal_scales(slice(0, 2))
+        deal_scales(slice(2, 3))
+        place_scales(second_planes, second_planes[:].bitcast(I32), range(1, QUADRANTS))
 
         banks = {}
         tiles = {}
-
-        first = {
-            "g": (xt, gate_planes, 0, wg, gate_planes, 2, FP4X4, "g", 2),
-            "a": (xt, gate_planes, 0, wa, mix_planes, 0, FP8X4, "ab", 3),
-            "b": (xq, mix_planes, 2, wc, mix_planes, 3, FP8X4, "ab", 3),
+        layer_1 = {
+            "g": (xt, gate_planes, 0, wg, gate_planes, 2, FP4X4, "gy", TILES),
+            "a": (xt, gate_planes, 0, wa, value_planes, 0, FP8X4, "ab", PRODUCT_BANKS),
+            "b": (xq, value_planes, 2, wc, value_planes, 3, FP8X4, "ab", PRODUCT_BANKS),
         }
 
         def first_product(name, tt):
-            x, x_planes, x_at, w, w_planes, w_at, w_dtype, tag, bufs = first[name]
+            x, x_planes, x_at, w, w_planes, w_at, w_dtype, tag, bufs = layer_1[name]
             bank = psum.tile([P, WIDE], F32, tag=tag, name=name, bufs=bufs)
             passes = x.shape[1]
             for z in range(passes):
@@ -129,27 +144,23 @@ def tile_mix_hidden_chosen_by_gate_pl_kernel(
                 )
             banks[name, tt] = bank
 
-        def dealt_read(bank):
-            return bank[:].rearrange("t (c e j) -> t c j e", j=PACK, e=4)
+        def in_natural(bank):
+            return bank[:].rearrange("t (c e j) -> t c j e", j=PACK, e=LINE_WORDS)
 
-        def dealt(tile):
-            return tile[:].rearrange("t j (c e) -> t c j e", e=4)
+        def in_dealt(tile):
+            return tile[:].rearrange("t j (c e) -> t c j e", e=LINE_WORDS)
 
         def gates(tt):
             first_product("g", tt)
             for name, sign in (("b", -1.0), ("a", 1.0)):
-                gate = work.tile([P, PACK, P], F32, tag="gate_" + name, name="gate_" + name, bufs=3)
-                nc.scalar.activation(out=dealt(gate), in_=dealt_read(banks["g", tt]), func=ACT.Sigmoid, scale=sign)
+                gate = work.tile([P, PACK, P], F32, tag="gate_" + name, name="gate_" + name, bufs=TILES)
+                nc.scalar.activation(out=in_dealt(gate), in_=in_natural(banks["g", tt]), func=ACT.Sigmoid, scale=sign)
                 tiles["gate", name, tt] = gate
 
-        def product(name, tt):
-            part = work.tile([P, PACK, P], F32, tag="part_" + name, name="part_" + name)
-            nc.vector.tensor_tensor(out=dealt(part), in0=dealt_read(banks[name, tt]), in1=dealt(tiles["gate", name, tt]), op=ALU.mult)
+        def gated(name, tt):
+            part = work.tile([P, PACK, P], F32, tag="part_" + name, name="part_" + name, bufs=PART_TILES)
+            nc.vector.tensor_tensor(out=in_dealt(part), in0=in_natural(banks[name, tt]), in1=in_dealt(tiles["gate", name, tt]), op=ALU.mult)
             tiles["part", name, tt] = part
-
-        def products(tt):
-            product("b", tt)
-            product("a", tt)
 
         def turn(tt):
             mix = psum.tile([P, PACK, P], F32, tag="mix", name="mix", bufs=1)
@@ -170,47 +181,37 @@ def tile_mix_hidden_chosen_by_gate_pl_kernel(
             tiles["hid", tt] = hid
 
         def quantise_hid(tt):
-            codes = work.tile([P, P], I32, tag="hid_codes", name="hid_codes", align_bytes=64, bufs=4)
-            scales = work.tile([P, P], U8, tag="hid_scales", name="hid_scales", align_bytes=64, bufs=4)
+            codes = work.tile([P, P], I32, tag="hid_codes", name="hid_codes", align_bytes=64, bufs=TILES)
+            scales = work.tile([P, P], U8, tag="hid_scales", name="hid_scales", align_bytes=64, bufs=TILES)
             nc.vector.quantize_mx(out=codes[:].bitcast(FP8X4), scales=scales[:], in_=tiles["hid", tt][:].rearrange("p t j -> p (t j)"))
             tiles["hid_codes", tt] = codes
             tiles["hid_scales", tt] = scales
 
-        def deal_words(at, raw, z):
-            nc.vector.tensor_copy(
-                out=second_words[:, at, :].rearrange("p (i c e) -> p c i e", i=PACK, e=4),
-                in_=raw[:, z, :].rearrange("p (c e i) -> p c i e", i=PACK, e=4),
-            )
-
         def second_layer(tt):
-            y = psum.tile([P, PACK, P], F32, tag="y", name="y", bufs=2)
-            cols = slice(P * tt, P * (tt + 1))
-            for z in range(3):
+            y = psum.tile([P, PACK, P], F32, tag="gy", name="y", bufs=TILES)
+            moving = [(xt[:, z, 2 * P * tt:2 * P * (tt + 1)].bitcast(FP4X4), gate_planes[:, z, P * tt:P * (tt + 1)]) for z in range(2)]
+            moving.append((tiles["hid_codes", tt][:].bitcast(FP8X4), tiles["hid_scales", tt][:]))
+            for z, (rhs, rhs_scale) in enumerate(moving):
                 for i in range(PACK):
-                    rows = slice(P * i, P * (i + 1))
-                    if z < 2:
-                        rhs = xt[:, z, 2 * P * tt:2 * P * (tt + 1)].bitcast(FP4X4)
-                        rhs_scale = gate_planes[:, z, cols]
-                    else:
-                        rhs = tiles["hid_codes", tt][:].bitcast(FP8X4)
-                        rhs_scale = tiles["hid_scales", tt][:]
+                    cols = slice(P * i, P * (i + 1))
                     nc.tensor.matmul_mx(
-                        out=y[:, i, :], lhsT=second_words[:, z, rows].bitcast(FP8X4), lhsT_scale=second_planes[:, z, rows],
-                        rhs=rhs, rhs_scale=rhs_scale, start=(z == 0 and i == 0), stop=(z == 2 and i == PACK - 1),
+                        out=y[:, i, :], lhsT=second_words[:, z, cols].bitcast(FP8X4), lhsT_scale=second_planes[:, z, cols],
+                        rhs=rhs, rhs_scale=rhs_scale, start=(z == 0 and i == 0), stop=(z == len(moving) - 1 and i == PACK - 1),
                     )
             banks["y", tt] = y
 
         out_rows = out_0.rearrange("(p i) t -> p i t", i=PACK)
+        codes_out = out_1[0].rearrange("p c r -> p (c r)").bitcast(I32)
 
         def store_y(tt):
-            y_sb = work.tile([P, PACK, P], F32, tag="y_sb", name="y_sb", bufs=4)
+            y_sb = work.tile([P, PACK, P], F32, tag="y_sb", name="y_sb", bufs=TILES)
             nc.scalar.copy(out=y_sb[:], in_=banks["y", tt][:])
             nc.sync.dma_start(out=out_rows[:, :, P * tt:P * (tt + 1)], in_=y_sb[:])
             tiles["y_sb", tt] = y_sb
 
-        def round_y(tt, from_psum):
+        def round_y(tt):
             y_bf = work.tile([P, P, PACK], BF16, tag="y_bf", name="y_bf", align_bytes=64)
-            if from_psum:
+            if tt < TILES - 2:
                 nc.scalar.copy(out=y_bf[:], in_=banks["y", tt][:].rearrange("p i t -> p t i"))
             else:
                 nc.vector.tensor_copy(out=y_bf[:], in_=tiles["y_sb", tt][:].rearrange("p i t -> p t i"))
@@ -219,59 +220,56 @@ def tile_mix_hidden_chosen_by_gate_pl_kernel(
         def quantise_y(tt):
             cols = slice(P * tt, P * (tt + 1))
             nc.vector.quantize_mx(out=y_codes[:, cols].bitcast(FP8X4), scales=y_scales[:, cols], in_=tiles["y_bf", tt][:].rearrange("p t i -> p (t i)"))
-
-        codes_out = out_1[0].rearrange("p c r -> p (c r)").bitcast(I32)
+            if tt % 2 == 1:
+                pair = slice(P * (tt - 1), P * (tt + 1))
+                nc.sync.dma_start(out=codes_out[:, pair], in_=y_codes[:, pair])
 
         gates(0)
         gates(1)
         first_product("b", 0)
         first_product("b", 1)
-        product("b", 0)
-        first_product("a", 0)
+        gated("b", 0)
         gates(2)
-        product("a", 0)
+        first_product("a", 0)
+        gated("b", 1)
+        gated("a", 0)
         first_product("a", 1)
-        products(1)
-        turn(0)
         first_product("b", 2)
-        first_product("a", 2)
-        round_hid(0)
-        deal_words(0, wy_raw, 0)
-        quantise_hid(0)
+        gated("a", 1)
         gates(3)
-        turn(1)
-        deal_words(1, wy_raw, 1)
-        products(2)
-        first_product("b", 3)
-        first_product("a", 3)
-        round_hid(1)
-        deal_words(2, wb_raw, 0)
-        quantise_hid(1)
-        second_layer(0)
-        store_y(0)
-        products(3)
-        turn(2)
-        round_hid(2)
-        round_y(0, True)
-        second_layer(1)
-        quantise_y(0)
-        quantise_hid(2)
-        store_y(1)
-        round_y(1, True)
-        turn(3)
-        round_hid(3)
-        quantise_y(1)
-        quantise_hid(3)
-        nc.sync.dma_start(out=codes_out[:, 0:2 * P], in_=y_codes[:, 0:2 * P])
-        second_layer(2)
-        store_y(2)
-        round_y(2, False)
-        second_layer(3)
-        store_y(3)
-        quantise_y(2)
-        round_y(3, False)
-        quantise_y(3)
-        nc.sync.dma_start(out=codes_out[:, 2 * P:4 * P], in_=y_codes[:, 2 * P:4 * P])
-        for q in range(4):
+        gated("b", 2)
+        deal_words(0, wy_raw, 0)
+
+        for step in range(TILES + 1):
+            summed, done = step - 1, step - 2
+            if step < TILES:
+                turn(step)
+            if step + 2 < TILES:
+                first_product("a", step + 2)
+            if step + 3 < TILES:
+                first_product("b", step + 3)
+            if step < TILES:
+                round_hid(step)
+                if step == 0:
+                    deal_words(1, wy_raw, 1)
+                elif step + 2 < TILES:
+                    gated("b", step + 2)
+                else:
+                    quantise_y(done)
+                quantise_hid(step)
+            if step == 0:
+                deal_words(2, wb_raw, 0)
+            if step + 2 < TILES:
+                gated("a", step + 2)
+            if summed >= 0:
+                second_layer(summed)
+                store_y(summed)
+            if step == TILES:
+                quantise_y(done)
+            if summed >= 0:
+                round_y(summed)
+        quantise_y(TILES - 1)
+
+        for q in range(QUADRANTS):
             queue = nc.scalar if q % 2 else nc.sync
             queue.dma_start(out=out_2[0, 4 * q:4 * q + 4, :].bitcast(I32), in_=y_scales[32 * q:32 * q + 4, :].bitcast(I32))

from contextlib import ExitStack

import concourse.mybir as mybir
from concourse.masks import make_identity

F32 = mybir.dt.float32
BF16 = mybir.dt.bfloat16
I32 = mybir.dt.int32
U8 = mybir.dt.uint8
FP8X4 = mybir.dt.float8_e4m3fn_x4
FP4X4 = mybir.dt.float4_e2m1fn_x4
ACT = mybir.ActivationFunctionType
ALU = mybir.AluOpType

K, L, T, R, N = 1024, 512, 512, 512, 512
FLOPS = 2 * T * (K * R + L * R + K * R + R * N + K * N)

P = 128
PACK = 4
WIDE = 512
TILES = T // P
SCALE_ROWS = 16
QUADRANTS = 4
LINE_WORDS = 4
LINE_BYTES = 16
WARM_PASSES = 20
PRODUCT_BANKS = 3
PART_TILES = 3


def tile_mix_hidden_chosen_by_gate_pl_kernel(
    tc, xt_words, xt_scales, wa_words, wa_scales, xq_words, xq_scales, wc_words, wc_scales,
    wg_words, wg_scales, us, wb_words, wb_scales, wy_words, wy_scales, out_0, out_1, out_2,
):
    nc = tc.nc
    with ExitStack() as ctx:
        keep = ctx.enter_context(tc.tile_pool(name="keep", bufs=1))
        work = ctx.enter_context(tc.tile_pool(name="work", bufs=2))
        psum = ctx.enter_context(tc.psum_pool(name="psum", bufs=1))
        ctx.enter_context(tc.manual_schedule())

        gate_stage = keep.tile([P, 4, WIDE // 4], I32)
        gate_planes = keep.tile([P, 4, WIDE], U8, align_bytes=64)
        value_planes = keep.tile([P, 4, WIDE], U8, align_bytes=64)
        second_stage = keep.tile([P, 3, WIDE], U8, align_bytes=64)
        second_planes = keep.tile([P, 3, WIDE], U8, align_bytes=64)
        warm_in = keep.tile([P, PACK * P], BF16, align_bytes=64)
        warm_codes = keep.tile([P, P], I32, align_bytes=64)
        warm_scales = keep.tile([P, P], U8, align_bytes=64)
        xt = keep.tile([P, 2, 2 * T], U8, align_bytes=64)
        wg = keep.tile([P, 2, 2 * R], U8, align_bytes=64)
        xq = keep.tile([P, 1, 2 * T], U8, align_bytes=64)
        wa = keep.tile([P, 2, R], I32, align_bytes=64)
        wc = keep.tile([P, 1, R], I32, align_bytes=64)
        wy_raw = keep.tile([P, 2, N], I32, align_bytes=64)
        wb_raw = keep.tile([P, 1, N], I32, align_bytes=64)
        second_words = keep.tile([P, 3, N], I32, align_bytes=64)
        us_sb = keep.tile([P, PACK], F32)
        ident = keep.tile([P, P], F32)
        y_codes = keep.tile([P, T], I32, align_bytes=64)
        y_scales = keep.tile([P, T], U8, align_bytes=64)

        def stage_scales(queue, rows, tensors):
            at = 0
            for scales in tensors:
                passes = scales.shape[0]
                queue.dma_start(out=rows[:, at:at + passes, :], in_=scales.rearrange("z q c -> q z c").bitcast(I32))
                at = at + passes

        def place_scales(planes, rows, quadrants):
            for q in quadrants:
                nc.sync.dma_start(out=planes[32 * q:32 * q + 4, :, :].bitcast(I32), in_=rows[4 * q:4 * q + 4, :, :])

        def load_fp4(tile, words):
            nc.sync.dma_start(out=tile[:].bitcast(I32), in_=words.rearrange("z p c -> p z c").bitcast(I32))

        def load_fp8(tile, words):
            nc.sync.dma_start(out=tile[:], in_=words.rearrange("z p c r -> p z (c r)").bitcast(I32))

        def deal_scales(passes):
            nc.vector.tensor_copy(
                out=second_planes[:, passes, :].rearrange("p z (i c e) -> p z c i e", i=PACK, e=LINE_BYTES),
                in_=second_stage[:, passes, :].rearrange("p z (c e i) -> p z c i e", i=PACK, e=LINE_BYTES),
            )

        def deal_words(at, raw, z):
            nc.vector.tensor_copy(
                out=second_words[:, at, :].rearrange("p (i c e) -> p c i e", i=PACK, e=LINE_WORDS),
                in_=raw[:, z, :].rearrange("p (c e i) -> p c i e", i=PACK, e=LINE_WORDS),
            )

        stage_scales(nc.sync, gate_stage[0:SCALE_ROWS], [xt_scales, wg_scales])
        nc.vector.memset(value_planes[:].bitcast(I32), 0)
        stage_scales(nc.sync, value_planes[0:SCALE_ROWS].bitcast(I32), [wa_scales, xq_scales, wc_scales])
        load_fp4(xt, xt_words)
        load_fp4(wg, wg_words)
        load_fp4(xq, xq_words)

        nc.vector.memset(warm_in[:].bitcast(I32), 0)
        nc.vector.memset(gate_planes[:].bitcast(I32), 0)
        nc.vector.quantize_mx(out=warm_codes[:].bitcast(FP8X4), scales=warm_scales[:], in_=warm_in[:])
        warm = psum.tile([P, PACK, P], F32, tag="mix", name="warm", bufs=1)
        for i in range(WARM_PASSES):
            nc.tensor.matmul_mx(
                out=warm[:, i % PACK, :], lhsT=warm_codes[:].bitcast(FP8X4), lhsT_scale=warm_scales[:],
                rhs=warm_codes[:].bitcast(FP8X4), rhs_scale=warm_scales[:], start=True, stop=True,
            )

        nc.gpsimd.memset(second_stage[:].bitcast(I32), 0)
        stage_scales(nc.gpsimd, second_stage[0:SCALE_ROWS].bitcast(I32), [wy_scales, wb_scales])
        make_identity(nc, ident[:])
        nc.gpsimd.dma_start(out=us_sb[:], in_=us.rearrange("(p j) o -> p (j o)", j=PACK))

        place_scales(gate_planes, gate_stage, range(QUADRANTS))
        load_fp8(wc, wc_words)
        place_scales(value_planes, value_planes[:].bitcast(I32), range(1, QUADRANTS))
        load_fp8(wa, wa_words)
        load_fp8(wy_raw, wy_words)
        load_fp8(wb_raw, wb_words)
        deal_scales(slice(0, 2))
        deal_scales(slice(2, 3))
        place_scales(second_planes, second_planes[:].bitcast(I32), range(1, QUADRANTS))

        banks = {}
        tiles = {}
        layer_1 = {
            "g": (xt, gate_planes, 0, wg, gate_planes, 2, FP4X4, "gy", TILES),
            "a": (xt, gate_planes, 0, wa, value_planes, 0, FP8X4, "ab", PRODUCT_BANKS),
            "b": (xq, value_planes, 2, wc, value_planes, 3, FP8X4, "ab", PRODUCT_BANKS),
        }

        def first_product(name, tt):
            x, x_planes, x_at, w, w_planes, w_at, w_dtype, tag, bufs = layer_1[name]
            bank = psum.tile([P, WIDE], F32, tag=tag, name=name, bufs=bufs)
            passes = x.shape[1]
            for z in range(passes):
                nc.tensor.matmul_mx(
                    out=bank[:],
                    lhsT=x[:, z, 2 * P * tt:2 * P * (tt + 1)].bitcast(FP4X4),
                    lhsT_scale=x_planes[:, x_at + z, P * tt:P * (tt + 1)],
                    rhs=w[:, z, :].bitcast(w_dtype),
                    rhs_scale=w_planes[:, w_at + z, :],
                    start=(z == 0), stop=(z == passes - 1),
                )
            banks[name, tt] = bank

        def in_natural(bank):
            return bank[:].rearrange("t (c e j) -> t c j e", j=PACK, e=LINE_WORDS)

        def in_dealt(tile):
            return tile[:].rearrange("t j (c e) -> t c j e", e=LINE_WORDS)

        def gates(tt):
            first_product("g", tt)
            for name, sign in (("b", -1.0), ("a", 1.0)):
                gate = work.tile([P, PACK, P], F32, tag="gate_" + name, name="gate_" + name, bufs=TILES)
                nc.scalar.activation(out=in_dealt(gate), in_=in_natural(banks["g", tt]), func=ACT.Sigmoid, scale=sign)
                tiles["gate", name, tt] = gate

        def gated(name, tt):
            part = work.tile([P, PACK, P], F32, tag="part_" + name, name="part_" + name, bufs=PART_TILES)
            nc.vector.tensor_tensor(out=in_dealt(part), in0=in_natural(banks[name, tt]), in1=in_dealt(tiles["gate", name, tt]), op=ALU.mult)
            tiles["part", name, tt] = part

        def turn(tt):
            mix = psum.tile([P, PACK, P], F32, tag="mix", name="mix", bufs=1)
            for name in ("b", "a"):
                for j in range(PACK):
                    nc.tensor.matmul(
                        out=mix[:, j, :], lhsT=tiles["part", name, tt][:, j, :], rhs=ident[:], is_transpose=True,
                        start=(name == "b" and j == 0), stop=(name == "a" and j == PACK - 1),
                    )
            banks["mix", tt] = mix

        def round_hid(tt):
            hid = work.tile([P, P, PACK], BF16, tag="hid", name="hid", align_bytes=64)
            nc.vector.tensor_tensor(
                out=hid[:], in0=banks["mix", tt][:].rearrange("p j t -> p t j"),
                in1=us_sb[:].unsqueeze(1).to_broadcast([P, P, PACK]), op=ALU.mult,
            )
            tiles["hid", tt] = hid

        def quantise_hid(tt):
            codes = work.tile([P, P], I32, tag="hid_codes", name="hid_codes", align_bytes=64, bufs=TILES)
            scales = work.tile([P, P], U8, tag="hid_scales", name="hid_scales", align_bytes=64, bufs=TILES)
            nc.vector.quantize_mx(out=codes[:].bitcast(FP8X4), scales=scales[:], in_=tiles["hid", tt][:].rearrange("p t j -> p (t j)"))
            tiles["hid_codes", tt] = codes
            tiles["hid_scales", tt] = scales

        def second_layer(tt):
            y = psum.tile([P, PACK, P], F32, tag="gy", name="y", bufs=TILES)
            moving = [(xt[:, z, 2 * P * tt:2 * P * (tt + 1)].bitcast(FP4X4), gate_planes[:, z, P * tt:P * (tt + 1)]) for z in range(2)]
            moving.append((tiles["hid_codes", tt][:].bitcast(FP8X4), tiles["hid_scales", tt][:]))
            for z, (rhs, rhs_scale) in enumerate(moving):
                for i in range(PACK):
                    cols = slice(P * i, P * (i + 1))
                    nc.tensor.matmul_mx(
                        out=y[:, i, :], lhsT=second_words[:, z, cols].bitcast(FP8X4), lhsT_scale=second_planes[:, z, cols],
                        rhs=rhs, rhs_scale=rhs_scale, start=(z == 0 and i == 0), stop=(z == len(moving) - 1 and i == PACK - 1),
                    )
            banks["y", tt] = y

        out_rows = out_0.rearrange("(p i) t -> p i t", i=PACK)
        codes_out = out_1[0].rearrange("p c r -> p (c r)").bitcast(I32)

        def store_y(tt):
            y_sb = work.tile([P, PACK, P], F32, tag="y_sb", name="y_sb", bufs=TILES)
            nc.scalar.copy(out=y_sb[:], in_=banks["y", tt][:])
            nc.sync.dma_start(out=out_rows[:, :, P * tt:P * (tt + 1)], in_=y_sb[:])
            tiles["y_sb", tt] = y_sb

        def round_y(tt):
            y_bf = work.tile([P, P, PACK], BF16, tag="y_bf", name="y_bf", align_bytes=64)
            if tt < TILES - 2:
                nc.scalar.copy(out=y_bf[:], in_=banks["y", tt][:].rearrange("p i t -> p t i"))
            else:
                nc.vector.tensor_copy(out=y_bf[:], in_=tiles["y_sb", tt][:].rearrange("p i t -> p t i"))
            tiles["y_bf", tt] = y_bf

        def quantise_y(tt):
            cols = slice(P * tt, P * (tt + 1))
            nc.vector.quantize_mx(out=y_codes[:, cols].bitcast(FP8X4), scales=y_scales[:, cols], in_=tiles["y_bf", tt][:].rearrange("p t i -> p (t i)"))
            if tt % 2 == 1:
                pair = slice(P * (tt - 1), P * (tt + 1))
                nc.sync.dma_start(out=codes_out[:, pair], in_=y_codes[:, pair])

        gates(0)
        gates(1)
        first_product("b", 0)
        first_product("b", 1)
        gated("b", 0)
        gates(2)
        first_product("a", 0)
        gated("b", 1)
        gated("a", 0)
        first_product("a", 1)
        first_product("b", 2)
        gated("a", 1)
        gates(3)
        gated("b", 2)
        deal_words(0, wy_raw, 0)

        for step in range(TILES + 1):
            summed, done = step - 1, step - 2
            if step < TILES:
                turn(step)
            if step + 2 < TILES:
                first_product("a", step + 2)
            if step + 3 < TILES:
                first_product("b", step + 3)
            if step < TILES:
                round_hid(step)
                if step == 0:
                    deal_words(1, wy_raw, 1)
                elif step + 2 < TILES:
                    gated("b", step + 2)
                else:
                    quantise_y(done)
                quantise_hid(step)
            if step == 0:
                deal_words(2, wb_raw, 0)
            if step + 2 < TILES:
                gated("a", step + 2)
            if summed >= 0:
                second_layer(summed)
                store_y(summed)
            if step == TILES:
                quantise_y(done)
            if summed >= 0:
                round_y(summed)
        quantise_y(TILES - 1)

        for q in range(QUADRANTS):
            queue = nc.scalar if q % 2 else nc.sync
            queue.dma_start(out=out_2[0, 4 * q:4 * q + 4, :].bitcast(I32), in_=y_scales[32 * q:32 * q + 4, :].bitcast(I32))
